import numpy as np
import ml_dtypes


def mxq(x, axis, fmt="e4m3"):
    dtype, down = {"e4m3": (ml_dtypes.float8_e4m3fn, 7), "e5m2": (ml_dtypes.float8_e5m2, 14)}[fmt]
    v = np.moveaxis(np.asarray(x, np.float32).astype(ml_dtypes.bfloat16).astype(np.float64), axis, -1)
    blocks = v.reshape(v.shape[:-1] + (-1, 32))
    amax = np.abs(blocks).max(-1, keepdims=True)
    byte = np.maximum(np.where(amax > 0, np.frexp(amax)[1] - 1 + 127, 0) - down, 1)
    scale = np.exp2(byte - 127.0)
    codes = (blocks / scale).astype(np.float32).astype(dtype).astype(np.float64)
    return np.moveaxis((codes * scale).reshape(v.shape), -1, axis)


WIDE = False


def mx_kscale(k):
    if not WIDE:
        return np.ones(k)
    levels = np.array([24, -24, 12, -12, 0])
    if k % 512:
        return np.exp2(np.random.permutation(np.resize(levels, k // 32))).repeat(32)
    a = np.empty((k // 512, 16))
    for p in range(k // 512):
        a[p, :8] = np.random.permutation(np.resize(levels, 8))
        for g in range(8):
            far = levels[np.abs(levels - a[p, g]) >= 10]
            a[p, g + 8] = far[np.random.randint(len(far))]
    return np.exp2(a.ravel()).repeat(32)


def f64(x):
    return np.asarray(x).astype(np.float64)


def striped(idx):
    return np.tile(idx.reshape(-1, 16).T, (8, 1)).astype(np.uint16)


def unstriped(offs):
    return offs[:16].T.reshape(-1).astype(np.int64)


E2M1 = np.array([0.0, 0.5, 1.0, 1.5, 2.0, 3.0, 4.0, 6.0, -0.0, -0.5, -1.0, -1.5, -2.0, -3.0, -4.0, -6.0])


def pack_weight(w, fmt):
    k, n = w.shape
    w = f64(np.asarray(w, np.float32).astype(ml_dtypes.bfloat16)).reshape(k // 32, 32, n)
    amax = np.abs(w).max(1)
    if fmt == "e4m3":
        byte = np.frexp(amax)[1] - 1 + 127 - 7
    else:
        mant, ex = np.frexp(amax / 6.0)
        byte = np.where(mant > 0.5, ex, ex - 1) + 127
    byte = np.clip(np.where(amax > 0, byte, 1), 1, 254)
    scaled = (w * np.exp2(127.0 - byte)[:, None, :]).reshape(k, n).astype(np.float32)
    by_word = np.ascontiguousarray(scaled.reshape(k // 512, 128, 4, n).transpose(0, 1, 3, 2))
    if fmt == "e4m3":
        words = by_word.astype(ml_dtypes.float8_e4m3fn).view(np.uint8)
    else:
        c = by_word.astype(ml_dtypes.float4_e2m1fn).view(np.uint8) & 0xF
        words = (c[..., 0::2] | (c[..., 1::2] << 4)).reshape(k // 512, 128, 2 * n)
    return np.ascontiguousarray(words), np.ascontiguousarray(byte.astype(np.uint8).reshape(k // 512, 16, n))


def unpack_weight(words, scales, fmt):
    g, _, n = scales.shape
    words = np.ascontiguousarray(words).reshape(g, 128, n, -1)
    if fmt == "e4m3":
        vals = words.view(ml_dtypes.float8_e4m3fn).astype(np.float64)
    else:
        nib = np.empty((g, 128, n, 4), np.uint8)
        nib[..., 0::2] = words & 0xF
        nib[..., 1::2] = words >> 4
        vals = E2M1[nib]
    vals = vals * np.repeat(np.exp2(scales.astype(np.float64) - 127.0), 8, axis=1)[..., None]
    return vals.transpose(0, 1, 3, 2).reshape(g * 512, n)


def pack_table4(v):
    words, scales = pack_weight(v, "e2m1")
    g, t = words.shape[0] // 2, v.shape[1]
    return np.ascontiguousarray(words.reshape(g, 2, 128, t, 2).transpose(0, 2, 3, 1, 4).reshape(g, 128, t, 4)), scales


def unpack_table4(words, scales):
    g, _, t, _ = words.shape
    return unpack_weight(words.reshape(g, 128, t, 2, 2).transpose(0, 3, 1, 2, 4).reshape(2 * g, 128, 2 * t), scales, "e2m1")


K, F, N, T, J = 1024, 512, 256, 4096, 2048


def setup_inputs():
    n = np.random.standard_normal
    s = mx_kscale(K)[:, None]
    u = mx_kscale(F)[:, None]
    p_tab = pack_table4(n((K, T)) * s)
    p_co = pack_weight(n((K, F)) / np.sqrt(K) / s, "e4m3")
    p_si = pack_weight(n((K, F)) / np.sqrt(K) / s, "e4m3")
    p_fb = pack_weight(np.abs(n((F, N))) / F / u, "e4m3")
    return {
        "tab_words": p_tab[0],
        "tab_scales": p_tab[1],
        "co_words": p_co[0],
        "co_scales": p_co[1],
        "si_words": p_si[0],
        "si_scales": p_si[1],
        "gn": (np.random.uniform(0.5, 2.0, F) * u[:, 0]).astype(np.float32),
        "fb_words": p_fb[0],
        "fb_scales": p_fb[1],
        "offs": striped(np.random.permutation(T)[:J]),
    }


def reference(tab_words, tab_scales, co_words, co_scales, si_words, si_scales, gn, fb_words, fb_scales, offs):
    idx = unstriped(offs)
    tab_ = unpack_table4(tab_words, tab_scales)[:, idx]
    co_ = unpack_weight(co_words, co_scales, "e4m3")
    si_ = unpack_weight(si_words, si_scales, "e4m3")
    re = co_.T @ tab_
    im = si_.T @ tab_
    h = f64(gn)[:, None] * np.sqrt((re) ** 2 + (im) ** 2)
    h_ = mxq(h, 0, "e4m3")
    fb_ = unpack_weight(fb_words, fb_scales, "e4m3")
    y = fb_.T @ h_
    return np.log(y + 1.0)

@@ -1,0 +1,221 @@
+from contextlib import ExitStack
+
+import concourse.mybir as mybir
+
+K, F, N, T, J = 1024, 512, 256, 4096, 2048
+FLOPS = 2 * 2 * K * F * J + 2 * F * N * J
+
+F32 = mybir.dt.float32
+BF16 = mybir.dt.bfloat16
+I32 = mybir.dt.int32
+U32 = mybir.dt.uint32
+U16 = mybir.dt.uint16
+U8 = mybir.dt.uint8
+FP8X4 = mybir.dt.float8_e4m3fn_x4
+FP4X4 = mybir.dt.float4_e2m1fn_x4
+ALU = mybir.AluOpType
+ACT = mybir.ActivationFunctionType
+
+P = 128
+PACK = 4
+PASSES = K // (P * PACK)
+JT = 512
+TILES = J // JT
+RUN = 2
+SIGN_COLS = 32
+VECTOR_SQUARES = ((2, 1), (3, 0), (3, 1), (3, 2))
+
+
+def tile_list_meltab_maglog_kernel(
+    tc, tab_words, tab_scales, co_words, co_scales, si_words, si_scales, gn, fb_words, fb_scales, offs, out
+):
+    nc = tc.nc
+    with ExitStack() as ctx:
+        keep = ctx.enter_context(tc.tile_pool(name="keep", bufs=1))
+        ring = ctx.enter_context(tc.tile_pool(name="ring", bufs=2))
+        psum = ctx.enter_context(tc.psum_pool(name="psum", bufs=1))
+
+        offsets = keep.tile([P, J // 16], U16, name="offsets")
+        nc.sync.dma_start(offsets[:], offs)
+
+        def load_weight_words(words):
+            raw = keep.tile([P, PASSES, F], I32, name="raw_words", tag="raw_words", align_bytes=64)
+            nc.sync.dma_start(raw[:], words.rearrange("a p f b -> p a (f b)").bitcast(I32))
+            return raw
+
+        def load_scale_rows(queue, plane, scales):
+            for q in range(4):
+                queue.dma_start(
+                    plane[:].bitcast(I32)[32 * q : 32 * q + 4],
+                    scales[:, 4 * q : 4 * q + 4, :].rearrange("a r c -> r a c").bitcast(I32),
+                )
+
+        table_scales = keep.tile([P, T], U8, name="table_scales", align_bytes=64)
+        nc.sync.dma_start(
+            table_scales[:].bitcast(I32)[0:32, :], tab_scales.rearrange("a q t -> (a q) t").bitcast(I32)
+        )
+        co_scales_raw = keep.tile([P, PASSES, F], U8, name="co_scales_raw", tag="raw_scales", align_bytes=64)
+        nc.gpsimd.memset(co_scales_raw[:].bitcast(I32), 0)
+        load_scale_rows(nc.scalar, co_scales_raw, co_scales)
+        co_raw = load_weight_words(co_words)
+        gain = keep.tile([P, PACK], F32, name="gain")
+        nc.sync.dma_start(gain[:], gn.rearrange("(p t) -> p t", t=PACK))
+        table = keep.tile([P, T], I32, name="table", align_bytes=64)
+        nc.sync.dma_start(table[:], tab_words[0].rearrange("p t b -> p (t b)").bitcast(I32))
+
+        nc.vector.memset(table_scales[:].bitcast(I32)[32:64, :], 0)
+        nc.vector.memset(table_scales[:].bitcast(I32)[64:P, :], 0)
+        frame_planes = keep.tile([P, PASSES, J], U8, name="frame_planes", align_bytes=64)
+        nc.vector.memset(frame_planes[:].bitcast(I32), 0)
+
+        zero_in = keep.tile([P, 1], F32, name="zero_in")
+        zero = keep.tile([P, 1], F32, name="zero")
+        nc.vector.memset(zero_in[:], 0.0)
+        nc.scalar.activation(zero[:], zero_in[:], ACT.Sqrt)
+
+        picked_scales = keep.tile([P, J], U8, name="picked_scales", align_bytes=64)
+
+        def list_slice(c):
+            return offsets[:, c * (JT // 16) : (c + 1) * (JT // 16)]
+
+        def gather_scales(c):
+            nc.vector.tensor_copy(picked_scales[:, c * JT : (c + 1) * JT], table_scales[:].indirect(list_slice(c)))
+
+        def place_scales(queue, j0, j1):
+            for a in range(PASSES):
+                for q in range(4):
+                    row = 16 * a + 4 * q
+                    queue.dma_start(
+                        frame_planes[:, a, j0:j1].bitcast(I32)[32 * q : 32 * q + 4, :],
+                        picked_scales[:, j0:j1].bitcast(I32)[row : row + 4, :],
+                    )
+
+        def permute_words(name, raw_words):
+            codes = keep.tile([P, PASSES, PACK, P], I32, name=name, tag=name, align_bytes=64)
+            nc.vector.tensor_copy(
+                codes[:].rearrange("p a t m -> p a m t"), raw_words[:].rearrange("p a (m t) -> p a m t", t=PACK)
+            )
+            return codes
+
+        def permute_scales(name, raw_scales):
+            plane = keep.tile([P, PASSES, PACK, P], U8, name=name, align_bytes=64)
+            nc.vector.tensor_copy(plane[:], raw_scales[:].rearrange("p a (m t) -> p a t m", t=PACK))
+            return plane
+
+        def gather_frames(c):
+            if c == 0:
+                picked = keep.tile([P, JT], U32, name="first_picked", tag="si_codes", align_bytes=64)
+            else:
+                picked = ring.tile([P, JT], U32, name="picked", align_bytes=64)
+            nc.vector.tensor_copy(picked[:], table[:].bitcast(U32).indirect(list_slice(c)))
+            frames = ring.tile([P, PASSES, 2 * JT], U8, name="frames", align_bytes=64)
+            nc.vector.tensor_copy(
+                frames[:].bitcast(U16), picked[:].bitcast(U16).rearrange("p (j d) -> p d j", d=PASSES)
+            )
+            return frames
+
+        gather_scales(0)
+        place_scales(nc.scalar, 0, JT)
+        co = (permute_words("co_codes", co_raw), permute_scales("co_plane", co_scales_raw))
+        si_scales_raw = keep.tile([P, PASSES, F], U8, name="si_scales_raw", tag="raw_scales", align_bytes=64)
+        nc.gpsimd.memset(si_scales_raw[:].bitcast(I32), 0)
+        load_scale_rows(nc.sync, si_scales_raw, si_scales)
+        si_raw = load_weight_words(si_words)
+        frames_next = gather_frames(0)
+        si = (permute_words("si_codes", si_raw), permute_scales("si_plane", si_scales_raw))
+        for c in range(1, TILES):
+            gather_scales(c)
+        place_scales(nc.sync, JT, J)
+
+        fb_codes = keep.tile([P, N], I32, name="fb_codes", tag="raw_words", align_bytes=64)
+        nc.sync.dma_start(fb_codes[:], fb_words[0].rearrange("p n b -> p (n b)").bitcast(I32))
+        fb_plane = keep.tile([P, 1, N], U8, name="fb_plane", tag="raw_scales", align_bytes=64)
+        nc.gpsimd.memset(fb_plane[:].bitcast(I32), 0)
+        load_scale_rows(nc.sync, fb_plane, fb_scales)
+
+        sign_col = keep.tile([P, PACK], F32, name="sign_col")
+        nc.vector.tensor_scalar(sign_col[:], gain[:], 0.0, 2.0, ALU.is_ge, ALU.mult)
+        signs = keep.tile([P, SIGN_COLS, PACK], BF16, name="signs", align_bytes=64)
+        nc.vector.tensor_scalar(
+            signs[:], sign_col[:].unsqueeze(1).to_broadcast([P, SIGN_COLS, PACK]), -1.0, None, ALU.add
+        )
+        sign_rows = signs[:].rearrange("p j t -> p (j t)").unsqueeze(1)
+        sign_rows = sign_rows.to_broadcast([P, JT // SIGN_COLS, SIGN_COLS * PACK])
+
+        def transform(bank, weight, frames, c, t):
+            codes, plane = weight
+            acc = psum.tile([P, JT], F32, name="acc", tag="bank%d" % bank)
+            for a in range(PASSES):
+                nc.tensor.matmul_mx(
+                    out=acc[:],
+                    lhsT=codes[:, a, t, :].bitcast(FP8X4),
+                    lhsT_scale=plane[:, a, t, :],
+                    rhs=frames[:, a, :].bitcast(FP4X4),
+                    rhs_scale=frame_planes[:, a, c * JT : (c + 1) * JT],
+                    start=(a == 0),
+                    stop=(a == PASSES - 1),
+                )
+            return acc
+
+        power = []
+        magnitude = []
+
+        def root(c, half):
+            cols = slice(half * (JT // 2), (half + 1) * (JT // 2))
+            nc.scalar.activation(
+                magnitude[c][:, cols, :].rearrange("p (u i) t -> p u t i", i=RUN),
+                power[c][:, :, cols].rearrange("p t (u i) -> p u t i", i=RUN),
+                ACT.Sqrt,
+                bias=zero[:],
+            )
+
+        for c in range(TILES):
+            frames = frames_next
+            if c + 1 < TILES:
+                frames_next = gather_frames(c + 1)
+            power.append(keep.tile([P, PACK, JT], F32, name="power", tag="power%d" % c))
+            magnitude.append(keep.tile([P, JT, PACK], BF16, name="magnitude", tag="magnitude%d" % c, align_bytes=64))
+            for t in range(PACK):
+                re = transform(2 * t, co, frames, c, t)
+                im = transform(2 * t + 1, si, frames, c, t)
+                g = gain[:, t : t + 1]
+                im_sq = ring.tile([P, JT], F32, name="im_sq", bufs=4)
+                nc.scalar.activation(power[c][:, t, :], re[:], ACT.Square, bias=zero[:], scale=g)
+                if (c, t) in VECTOR_SQUARES:
+                    im_g = ring.tile([P, JT], F32, name="im_g")
+                    nc.vector.tensor_scalar(im_g[:], im[:], g, None, ALU.mult)
+                    nc.vector.tensor_tensor(im_sq[:], im_g[:], im_g[:], ALU.mult)
+                else:
+                    nc.scalar.activation(im_sq[:], im[:], ACT.Square, bias=zero[:], scale=g)
+                nc.vector.tensor_tensor(power[c][:, t, :], power[c][:, t, :], im_sq[:], ALU.add)
+                if c > 0 and t % 2 == 1:
+                    root(c - 1, t // 2)
+        root(TILES - 1, 0)
+        root(TILES - 1, 1)
+
+        result = keep.tile([P, N // P, J], F32, name="result", tag="power%d" % (TILES - 1))
+        for c in range(TILES):
+            h = ring.tile([P, JT * PACK], BF16, name="h", align_bytes=64)
+            nc.vector.tensor_tensor(
+                h[:].rearrange("p (u x) -> p u x", x=SIGN_COLS * PACK),
+                magnitude[c][:].rearrange("p (u j) t -> p u (j t)", j=SIGN_COLS),
+                sign_rows,
+                ALU.mult,
+            )
+            h_codes = ring.tile([P, JT], U32, name="h_codes", align_bytes=64, bufs=4)
+            h_plane = ring.tile([P, JT], U8, name="h_plane", align_bytes=64, bufs=4)
+            nc.vector.quantize_mx(out=h_codes[:].bitcast(FP8X4), scales=h_plane[:], in_=h[:])
+            for n in range(N // P):
+                y = psum.tile([P, JT], F32, name="y", tag="bank%d" % (2 * c + n))
+                nc.tensor.matmul_mx(
+                    out=y[:],
+                    lhsT=fb_codes[:, n * P : (n + 1) * P].bitcast(FP8X4),
+                    lhsT_scale=fb_plane[:, 0, n * P : (n + 1) * P],
+                    rhs=h_codes[:].bitcast(FP8X4),
+                    rhs_scale=h_plane[:],
+                    start=True,
+                    stop=True,
+                )
+                cols = slice(c * JT, (c + 1) * JT)
+                nc.scalar.activation(result[:, n, cols], y[:], ACT.Ln, bias=1.0)
+                nc.sync.dma_start(out[n * P : (n + 1) * P, cols], result[:, n, cols])

@@ -23,7 +23,10 @@ JT = 512
 TILES = J // JT
 RUN = 2
 SIGN_COLS = 32
-VECTOR_SQUARES = ((2, 1), (3, 0), (3, 1), (3, 2))
+FRAMES_AT = 2 * F
+FB_AT = FRAMES_AT + JT
+FIRST_W = FB_AT + N
+VECTOR_SQUARES = ((1, 1), (1, 2), (2, 1), (2, 2), (3, 0), (3, 1))
 
 
 def tile_list_meltab_maglog_kernel(
@@ -38,75 +41,66 @@ def tile_list_meltab_maglog_kernel(
         offsets = keep.tile([P, J // 16], U16, name="offsets")
         nc.sync.dma_start(offsets[:], offs)
 
-        def load_weight_words(words):
-            raw = keep.tile([P, PASSES, F], I32, name="raw_words", tag="raw_words", align_bytes=64)
-            nc.sync.dma_start(raw[:], words.rearrange("a p f b -> p a (f b)").bitcast(I32))
-            return raw
+        rows = slice(96, P)
 
-        def load_scale_rows(queue, plane, scales):
-            for q in range(4):
-                queue.dma_start(
-                    plane[:].bitcast(I32)[32 * q : 32 * q + 4],
-                    scales[:, 4 * q : 4 * q + 4, :].rearrange("a r c -> r a c").bitcast(I32),
-                )
+        def words_view(words):
+            return words.rearrange("a p f b -> p a (f b)").bitcast(I32)
+
+        def rows_view(scales):
+            return scales.rearrange("a q c -> (a q) c").bitcast(I32)
 
         table_scales = keep.tile([P, T], U8, name="table_scales", align_bytes=64)
-        nc.sync.dma_start(
-            table_scales[:].bitcast(I32)[0:32, :], tab_scales.rearrange("a q t -> (a q) t").bitcast(I32)
-        )
-        co_scales_raw = keep.tile([P, PASSES, F], U8, name="co_scales_raw", tag="raw_scales", align_bytes=64)
-        nc.gpsimd.memset(co_scales_raw[:].bitcast(I32), 0)
-        load_scale_rows(nc.scalar, co_scales_raw, co_scales)
-        co_raw = load_weight_words(co_words)
+        nc.sync.dma_start(table_scales[:].bitcast(I32)[rows, :], rows_view(tab_scales))
+        weight_scales = keep.tile([P, 2, F], U8, name="weight_scales", align_bytes=64)
+        nc.sync.dma_start(weight_scales[:, 0, :].bitcast(I32)[rows, :], rows_view(co_scales))
+        nc.sync.dma_start(weight_scales[:, 1, :].bitcast(I32)[rows, :], rows_view(si_scales))
+        first_rows = keep.tile([P, FIRST_W], U8, name="first_rows", align_bytes=64)
+        nc.sync.dma_start(first_rows[:, FB_AT:].bitcast(I32)[96:112, :], rows_view(fb_scales))
         gain = keep.tile([P, PACK], F32, name="gain")
         nc.sync.dma_start(gain[:], gn.rearrange("(p t) -> p t", t=PACK))
+        co_raw = keep.tile([P, PASSES, F], I32, name="co_raw", tag="staging", align_bytes=64)
+        nc.sync.dma_start(co_raw[:], words_view(co_words))
         table = keep.tile([P, T], I32, name="table", align_bytes=64)
         nc.sync.dma_start(table[:], tab_words[0].rearrange("p t b -> p (t b)").bitcast(I32))
 
-        nc.vector.memset(table_scales[:].bitcast(I32)[32:64, :], 0)
-        nc.vector.memset(table_scales[:].bitcast(I32)[64:P, :], 0)
-        frame_planes = keep.tile([P, PASSES, J], U8, name="frame_planes", align_bytes=64)
-        nc.vector.memset(frame_planes[:].bitcast(I32), 0)
+        nc.vector.memset(table_scales[:].bitcast(I32)[0:96, :], 0)
+        nc.gpsimd.memset(weight_scales[:].bitcast(I32)[0:96], 0)
+        first_planes = keep.tile([P, PASSES, FIRST_W], U8, name="first_planes", align_bytes=64)
+        middle_planes = keep.tile([P, PASSES, 2 * JT], U8, name="middle_planes", align_bytes=64)
+        last_planes = keep.tile([P, PASSES, JT], U8, name="last_planes", align_bytes=64)
+        nc.gpsimd.memset(first_planes[:].bitcast(I32), 0)
+        nc.gpsimd.memset(middle_planes[:].bitcast(I32), 0)
+        nc.gpsimd.memset(last_planes[:].bitcast(I32), 0)
 
         zero_in = keep.tile([P, 1], F32, name="zero_in")
         zero = keep.tile([P, 1], F32, name="zero")
         nc.vector.memset(zero_in[:], 0.0)
         nc.scalar.activation(zero[:], zero_in[:], ACT.Sqrt)
 
-        picked_scales = keep.tile([P, J], U8, name="picked_scales", align_bytes=64)
-
         def list_slice(c):
             return offsets[:, c * (JT // 16) : (c + 1) * (JT // 16)]
 
-        def gather_scales(c):
-            nc.vector.tensor_copy(picked_scales[:, c * JT : (c + 1) * JT], table_scales[:].indirect(list_slice(c)))
+        def gather_scales(dst, c):
+            nc.vector.tensor_copy(dst, table_scales[:].indirect(list_slice(c)))
 
-        def place_scales(queue, j0, j1):
+        def place_rows(queue, planes, source, widths):
             for a in range(PASSES):
                 for q in range(4):
-                    row = 16 * a + 4 * q
+                    row = 96 + 16 * a + 4 * q
                     queue.dma_start(
-                        frame_planes[:, a, j0:j1].bitcast(I32)[32 * q : 32 * q + 4, :],
-                        picked_scales[:, j0:j1].bitcast(I32)[row : row + 4, :],
+                        planes[:, a, : widths[a]].bitcast(I32)[32 * q : 32 * q + 4, :],
+                        source[:, : widths[a]].bitcast(I32)[row : row + 4, :],
                     )
 
         def permute_words(name, raw_words):
-            codes = keep.tile([P, PASSES, PACK, P], I32, name=name, tag=name, align_bytes=64)
+            codes = keep.tile([P, PASSES, PACK, P], I32, name=name, align_bytes=64)
             nc.vector.tensor_copy(
                 codes[:].rearrange("p a t m -> p a m t"), raw_words[:].rearrange("p a (m t) -> p a m t", t=PACK)
             )
             return codes
 
-        def permute_scales(name, raw_scales):
-            plane = keep.tile([P, PASSES, PACK, P], U8, name=name, align_bytes=64)
-            nc.vector.tensor_copy(plane[:], raw_scales[:].rearrange("p a (m t) -> p a t m", t=PACK))
-            return plane
-
         def gather_frames(c):
-            if c == 0:
-                picked = keep.tile([P, JT], U32, name="first_picked", tag="si_codes", align_bytes=64)
-            else:
-                picked = ring.tile([P, JT], U32, name="picked", align_bytes=64)
+            picked = ring.tile([P, JT], U32, name="picked", align_bytes=64, bufs=1)
             nc.vector.tensor_copy(picked[:], table[:].bitcast(U32).indirect(list_slice(c)))
             frames = ring.tile([P, PASSES, 2 * JT], U8, name="frames", align_bytes=64)
             nc.vector.tensor_copy(
@@ -114,24 +108,33 @@ def tile_list_meltab_maglog_kernel(
             )
             return frames
 
-        gather_scales(0)
-        place_scales(nc.scalar, 0, JT)
-        co = (permute_words("co_codes", co_raw), permute_scales("co_plane", co_scales_raw))
-        si_scales_raw = keep.tile([P, PASSES, F], U8, name="si_scales_raw", tag="raw_scales", align_bytes=64)
-        nc.gpsimd.memset(si_scales_raw[:].bitcast(I32), 0)
-        load_scale_rows(nc.sync, si_scales_raw, si_scales)
-        si_raw = load_weight_words(si_words)
+        first_scales = keep.tile([P, JT], U8, name="first_scales", align_bytes=64)
+        gather_scales(first_scales[:], 0)
+        nc.vector.tensor_copy(
+            first_rows[:, : 2 * F].rearrange("p (w t m) -> p w t m", w=2, t=PACK),
+            weight_scales[:].rearrange("p w (m t) -> p w t m", t=PACK),
+        )
+        nc.vector.tensor_copy(
+            first_rows[:, FRAMES_AT:FB_AT].bitcast(I32)[rows, :], first_scales[:].bitcast(I32)[rows, :]
+        )
+        place_rows(nc.scalar, first_planes, first_rows, (FIRST_W, FB_AT))
+        co_codes = permute_words("co_codes", co_raw)
+        si_raw = keep.tile([P, PASSES, F], I32, name="si_raw", tag="staging", align_bytes=64)
+        nc.sync.dma_start(si_raw[:], words_view(si_words))
         frames_next = gather_frames(0)
-        si = (permute_words("si_codes", si_raw), permute_scales("si_plane", si_scales_raw))
-        for c in range(1, TILES):
-            gather_scales(c)
-        place_scales(nc.sync, JT, J)
+        si_codes = permute_words("si_codes", si_raw)
+        middle_scales = keep.tile([P, 2 * JT], U8, name="middle_scales", align_bytes=64)
+        for c in (1, 2):
+            gather_scales(middle_scales[:, (c - 1) * JT : c * JT], c)
+        place_rows(nc.sync, middle_planes, middle_scales, (2 * JT, 2 * JT))
+        last_scales = keep.tile([P, JT], U8, name="last_scales", tag="staging", align_bytes=64)
+        gather_scales(last_scales[:], 3)
+        place_rows(nc.sync, last_planes, last_scales, (JT, JT))
+        co = (co_codes, 0)
+        si = (si_codes, F)
 
-        fb_codes = keep.tile([P, N], I32, name="fb_codes", tag="raw_words", align_bytes=64)
+        fb_codes = keep.tile([P, N], I32, name="fb_codes", tag="staging", align_bytes=64)
         nc.sync.dma_start(fb_codes[:], fb_words[0].rearrange("p n b -> p (n b)").bitcast(I32))
-        fb_plane = keep.tile([P, 1, N], U8, name="fb_plane", tag="raw_scales", align_bytes=64)
-        nc.gpsimd.memset(fb_plane[:].bitcast(I32), 0)
-        load_scale_rows(nc.sync, fb_plane, fb_scales)
 
         sign_col = keep.tile([P, PACK], F32, name="sign_col")
         nc.vector.tensor_scalar(sign_col[:], gain[:], 0.0, 2.0, ALU.is_ge, ALU.mult)
@@ -143,15 +146,21 @@ def tile_list_meltab_maglog_kernel(
         sign_rows = sign_rows.to_broadcast([P, JT // SIGN_COLS, SIGN_COLS * PACK])
 
         def transform(bank, weight, frames, c, t):
-            codes, plane = weight
+            codes, at = weight
             acc = psum.tile([P, JT], F32, name="acc", tag="bank%d" % bank)
             for a in range(PASSES):
+                if c == 0:
+                    frame_plane = first_planes[:, a, FRAMES_AT:FB_AT]
+                elif c < 3:
+                    frame_plane = middle_planes[:, a, (c - 1) * JT : c * JT]
+                else:
+                    frame_plane = last_planes[:, a, :]
                 nc.tensor.matmul_mx(
                     out=acc[:],
                     lhsT=codes[:, a, t, :].bitcast(FP8X4),
-                    lhsT_scale=plane[:, a, t, :],
+                    lhsT_scale=first_planes[:, a, at + t * P : at + (t + 1) * P],
                     rhs=frames[:, a, :].bitcast(FP4X4),
-                    rhs_scale=frame_planes[:, a, c * JT : (c + 1) * JT],
+                    rhs_scale=frame_plane,
                     start=(a == 0),
                     stop=(a == PASSES - 1),
                 )
@@ -175,12 +184,20 @@ def tile_list_meltab_maglog_kernel(
                 frames_next = gather_frames(c + 1)
             power.append(keep.tile([P, PACK, JT], F32, name="power", tag="power%d" % c))
             magnitude.append(keep.tile([P, JT, PACK], BF16, name="magnitude", tag="magnitude%d" % c, align_bytes=64))
-            for t in range(PACK):
+
+            def square_re(t):
                 re = transform(2 * t, co, frames, c, t)
+                nc.scalar.activation(power[c][:, t, :], re[:], ACT.Square, bias=zero[:], scale=gain[:, t : t + 1])
+
+            if c == 0:
+                for t in range(PACK):
+                    square_re(t)
+            for t in range(PACK):
+                if c > 0:
+                    square_re(t)
                 im = transform(2 * t + 1, si, frames, c, t)
                 g = gain[:, t : t + 1]
                 im_sq = ring.tile([P, JT], F32, name="im_sq", bufs=4)
-                nc.scalar.activation(power[c][:, t, :], re[:], ACT.Square, bias=zero[:], scale=g)
                 if (c, t) in VECTOR_SQUARES:
                     im_g = ring.tile([P, JT], F32, name="im_g")
                     nc.vector.tensor_scalar(im_g[:], im[:], g, None, ALU.mult)
@@ -188,10 +205,11 @@ def tile_list_meltab_maglog_kernel(
                 else:
                     nc.scalar.activation(im_sq[:], im[:], ACT.Square, bias=zero[:], scale=g)
                 nc.vector.tensor_tensor(power[c][:, t, :], power[c][:, t, :], im_sq[:], ALU.add)
-                if c > 0 and t % 2 == 1:
+                if 0 < c < TILES - 1 and t % 2 == 1:
                     root(c - 1, t // 2)
-        root(TILES - 1, 0)
-        root(TILES - 1, 1)
+        for c in (TILES - 2, TILES - 1):
+            root(c, 0)
+            root(c, 1)
 
         result = keep.tile([P, N // P, J], F32, name="result", tag="power%d" % (TILES - 1))
         for c in range(TILES):
@@ -210,7 +228,7 @@ def tile_list_meltab_maglog_kernel(
                 nc.tensor.matmul_mx(
                     out=y[:],
                     lhsT=fb_codes[:, n * P : (n + 1) * P].bitcast(FP8X4),
-                    lhsT_scale=fb_plane[:, 0, n * P : (n + 1) * P],
+                    lhsT_scale=first_planes[:, 0, FB_AT + n * P : FB_AT + (n + 1) * P],
                     rhs=h_codes[:].bitcast(FP8X4),
                     rhs_scale=h_plane[:],
                     start=True,

@@ -26,7 +26,7 @@ SIGN_COLS = 32
 FRAMES_AT = 2 * F
 FB_AT = FRAMES_AT + JT
 FIRST_W = FB_AT + N
-VECTOR_SQUARES = ((1, 1), (1, 2), (2, 1), (2, 2), (3, 0), (3, 1))
+VECTOR_PAIRS = ((0, 0), (2, 0), (2, 1))
 
 
 def tile_list_meltab_maglog_kernel(
@@ -145,9 +145,8 @@ def tile_list_meltab_maglog_kernel(
         sign_rows = signs[:].rearrange("p j t -> p (j t)").unsqueeze(1)
         sign_rows = sign_rows.to_broadcast([P, JT // SIGN_COLS, SIGN_COLS * PACK])
 
-        def transform(bank, weight, frames, c, t):
+        def transform(acc, weight, frames, c, t):
             codes, at = weight
-            acc = psum.tile([P, JT], F32, name="acc", tag="bank%d" % bank)
             for a in range(PASSES):
                 if c == 0:
                     frame_plane = first_planes[:, a, FRAMES_AT:FB_AT]
@@ -156,7 +155,7 @@ def tile_list_meltab_maglog_kernel(
                 else:
                     frame_plane = last_planes[:, a, :]
                 nc.tensor.matmul_mx(
-                    out=acc[:],
+                    out=acc,
                     lhsT=codes[:, a, t, :].bitcast(FP8X4),
                     lhsT_scale=first_planes[:, a, at + t * P : at + (t + 1) * P],
                     rhs=frames[:, a, :].bitcast(FP4X4),
@@ -164,8 +163,8 @@ def tile_list_meltab_maglog_kernel(
                     start=(a == 0),
                     stop=(a == PASSES - 1),
                 )
-            return acc
 
+        squares = []
         power = []
         magnitude = []
 
@@ -178,35 +177,43 @@ def tile_list_meltab_maglog_kernel(
                 bias=zero[:],
             )
 
+        def square(dst, src, t):
+            nc.scalar.activation(dst, src, ACT.Square, scale=gain[:, t : t + 1])
+
         for c in range(TILES):
             frames = frames_next
             if c + 1 < TILES:
                 frames_next = gather_frames(c + 1)
+            sq = keep.tile([P, PACK, 2, JT], F32, name="sq", tag="squares%d" % (c % 2))
             power.append(keep.tile([P, PACK, JT], F32, name="power", tag="power%d" % c))
             magnitude.append(keep.tile([P, JT, PACK], BF16, name="magnitude", tag="magnitude%d" % c, align_bytes=64))
-
-            def square_re(t):
-                re = transform(2 * t, co, frames, c, t)
-                nc.scalar.activation(power[c][:, t, :], re[:], ACT.Square, bias=zero[:], scale=gain[:, t : t + 1])
-
+            re = [psum.tile([P, JT], F32, name="re", tag="bank%d" % (2 * t))[:] for t in range(PACK)]
+            im = [psum.tile([P, JT], F32, name="im", tag="bank%d" % (2 * t + 1))[:] for t in range(PACK)]
             if c == 0:
                 for t in range(PACK):
-                    square_re(t)
-            for t in range(PACK):
-                if c > 0:
-                    square_re(t)
-                im = transform(2 * t + 1, si, frames, c, t)
-                g = gain[:, t : t + 1]
-                im_sq = ring.tile([P, JT], F32, name="im_sq", bufs=4)
-                if (c, t) in VECTOR_SQUARES:
-                    im_g = ring.tile([P, JT], F32, name="im_g")
-                    nc.vector.tensor_scalar(im_g[:], im[:], g, None, ALU.mult)
-                    nc.vector.tensor_tensor(im_sq[:], im_g[:], im_g[:], ALU.mult)
-                else:
-                    nc.scalar.activation(im_sq[:], im[:], ACT.Square, bias=zero[:], scale=g)
-                nc.vector.tensor_tensor(power[c][:, t, :], power[c][:, t, :], im_sq[:], ALU.add)
-                if 0 < c < TILES - 1 and t % 2 == 1:
-                    root(c - 1, t // 2)
+                    transform(re[t], co, frames, c, t)
+                    square(sq[:, t, 0, :], re[t], t)
+            for u in range(PACK // 2):
+                pair = (2 * u, 2 * u + 1)
+                both = slice(2 * u, 2 * u + 2)
+                for t in pair:
+                    if c > 0:
+                        transform(re[t], co, frames, c, t)
+                    transform(im[t], si, frames, c, t)
+                on_vector = (c, u) in VECTOR_PAIRS
+                if on_vector:
+                    im_g = ring.tile([P, 2, JT], F32, name="im_g")
+                    for t in pair:
+                        nc.vector.tensor_scalar(im_g[:, t % 2, :], im[t], gain[:, t : t + 1], None, ALU.mult)
+                    nc.vector.tensor_tensor(sq[:, both, 1, :], im_g[:], im_g[:], ALU.mult)
+                for t in (pair if c == 0 else reversed(pair)):
+                    if not on_vector:
+                        square(sq[:, t, 1, :], im[t], t)
+                    if c > 0:
+                        square(sq[:, t, 0, :], re[t], t)
+                nc.vector.tensor_tensor(power[c][:, both, :], sq[:, both, 0, :], sq[:, both, 1, :], ALU.add)
+                if 0 < c < TILES - 1:
+                    root(c - 1, u)
         for c in (TILES - 2, TILES - 1):
             root(c, 0)
             root(c, 1)
@@ -223,10 +230,10 @@ def tile_list_meltab_maglog_kernel(
             h_codes = ring.tile([P, JT], U32, name="h_codes", align_bytes=64, bufs=4)
             h_plane = ring.tile([P, JT], U8, name="h_plane", align_bytes=64, bufs=4)
             nc.vector.quantize_mx(out=h_codes[:].bitcast(FP8X4), scales=h_plane[:], in_=h[:])
+            ys = [psum.tile([P, JT], F32, name="y", tag="bank%d" % (2 * c + n))[:] for n in range(N // P)]
             for n in range(N // P):
-                y = psum.tile([P, JT], F32, name="y", tag="bank%d" % (2 * c + n))
                 nc.tensor.matmul_mx(
-                    out=y[:],
+                    out=ys[n],
                     lhsT=fb_codes[:, n * P : (n + 1) * P].bitcast(FP8X4),
                     lhsT_scale=first_planes[:, 0, FB_AT + n * P : FB_AT + (n + 1) * P],
                     rhs=h_codes[:].bitcast(FP8X4),
@@ -234,6 +241,7 @@ def tile_list_meltab_maglog_kernel(
                     start=True,
                     stop=True,
                 )
-                cols = slice(c * JT, (c + 1) * JT)
-                nc.scalar.activation(result[:, n, cols], y[:], ACT.Ln, bias=1.0)
+            cols = slice(c * JT, (c + 1) * JT)
+            for n in reversed(range(N // P)):
+                nc.scalar.activation(result[:, n, cols], ys[n], ACT.Ln, bias=1.0)
                 nc.sync.dma_start(out[n * P : (n + 1) * P, cols], result[:, n, cols])

@@ -26,7 +26,7 @@ SIGN_COLS = 32
 FRAMES_AT = 2 * F
 FB_AT = FRAMES_AT + JT
 FIRST_W = FB_AT + N
-VECTOR_PAIRS = ((0, 0), (2, 0), (2, 1))
+VECTOR_PAIRS = ((1, 1), (2, 1), (3, 0))
 
 
 def tile_list_meltab_maglog_kernel(
@@ -94,9 +94,11 @@ def tile_list_meltab_maglog_kernel(
 
         def permute_words(name, raw_words):
             codes = keep.tile([P, PASSES, PACK, P], I32, name=name, align_bytes=64)
-            nc.vector.tensor_copy(
-                codes[:].rearrange("p a t m -> p a m t"), raw_words[:].rearrange("p a (m t) -> p a m t", t=PACK)
-            )
+            for a in range(PASSES):
+                nc.vector.tensor_copy(
+                    codes[:, a].rearrange("p t (u i) -> p u t i", i=4),
+                    raw_words[:, a].rearrange("p (u i t) -> p u t i", i=4, t=PACK),
+                )
             return codes
 
         def gather_frames(c):
@@ -171,8 +173,8 @@ def tile_list_meltab_maglog_kernel(
         def root(c, half):
             cols = slice(half * (JT // 2), (half + 1) * (JT // 2))
             nc.scalar.activation(
-                magnitude[c][:, cols, :].rearrange("p (u i) t -> p u t i", i=RUN),
-                power[c][:, :, cols].rearrange("p t (u i) -> p u t i", i=RUN),
+                magnitude[c][:, cols, :].rearrange("p j (u e) -> p j u e", e=2),
+                power[c][:, :, cols, :].rearrange("p u j e -> p j u e"),
                 ACT.Sqrt,
                 bias=zero[:],
             )
@@ -185,7 +187,7 @@ def tile_list_meltab_maglog_kernel(
             if c + 1 < TILES:
                 frames_next = gather_frames(c + 1)
             sq = keep.tile([P, PACK, 2, JT], F32, name="sq", tag="squares%d" % (c % 2))
-            power.append(keep.tile([P, PACK, JT], F32, name="power", tag="power%d" % c))
+            power.append(keep.tile([P, PACK // 2, JT, 2], F32, name="power", tag="power%d" % c))
             magnitude.append(keep.tile([P, JT, PACK], BF16, name="magnitude", tag="magnitude%d" % c, align_bytes=64))
             re = [psum.tile([P, JT], F32, name="re", tag="bank%d" % (2 * t))[:] for t in range(PACK)]
             im = [psum.tile([P, JT], F32, name="im", tag="bank%d" % (2 * t + 1))[:] for t in range(PACK)]
@@ -211,7 +213,12 @@ def tile_list_meltab_maglog_kernel(
                         square(sq[:, t, 1, :], im[t], t)
                     if c > 0:
                         square(sq[:, t, 0, :], re[t], t)
-                nc.vector.tensor_tensor(power[c][:, both, :], sq[:, both, 0, :], sq[:, both, 1, :], ALU.add)
+                nc.vector.tensor_tensor(
+                    power[c][:, u].rearrange("p (v i) e -> p v e i", i=RUN),
+                    sq[:, both, 0, :].rearrange("p e (v i) -> p v e i", i=RUN),
+                    sq[:, both, 1, :].rearrange("p e (v i) -> p v e i", i=RUN),
+                    ALU.add,
+                )
                 if 0 < c < TILES - 1:
                     root(c - 1, u)
         for c in (TILES - 2, TILES - 1):

@@ -24,9 +24,8 @@ TILES = J // JT
 RUN = 2
 SIGN_COLS = 32
 FRAMES_AT = 2 * F
-FB_AT = FRAMES_AT + JT
-FIRST_W = FB_AT + N
-VECTOR_PAIRS = ((1, 1), (2, 1), (3, 0))
+FIRST_W = FRAMES_AT + JT
+VECTOR_SQUARES = ((1, 3), (2, 2), (2, 3), (3, 0), (3, 1))
 
 
 def tile_list_meltab_maglog_kernel(
@@ -35,13 +34,14 @@ def tile_list_meltab_maglog_kernel(
     nc = tc.nc
     with ExitStack() as ctx:
         keep = ctx.enter_context(tc.tile_pool(name="keep", bufs=1))
+        handed = ctx.enter_context(tc.tile_pool(name="handed", bufs=1))
         ring = ctx.enter_context(tc.tile_pool(name="ring", bufs=2))
         psum = ctx.enter_context(tc.psum_pool(name="psum", bufs=1))
 
         offsets = keep.tile([P, J // 16], U16, name="offsets")
         nc.sync.dma_start(offsets[:], offs)
 
-        rows = slice(96, P)
+        rows = slice(0, 32)
 
         def words_view(words):
             return words.rearrange("a p f b -> p a (f b)").bitcast(I32)
@@ -54,8 +54,6 @@ def tile_list_meltab_maglog_kernel(
         weight_scales = keep.tile([P, 2, F], U8, name="weight_scales", align_bytes=64)
         nc.sync.dma_start(weight_scales[:, 0, :].bitcast(I32)[rows, :], rows_view(co_scales))
         nc.sync.dma_start(weight_scales[:, 1, :].bitcast(I32)[rows, :], rows_view(si_scales))
-        first_rows = keep.tile([P, FIRST_W], U8, name="first_rows", align_bytes=64)
-        nc.sync.dma_start(first_rows[:, FB_AT:].bitcast(I32)[96:112, :], rows_view(fb_scales))
         gain = keep.tile([P, PACK], F32, name="gain")
         nc.sync.dma_start(gain[:], gn.rearrange("(p t) -> p t", t=PACK))
         co_raw = keep.tile([P, PASSES, F], I32, name="co_raw", tag="staging", align_bytes=64)
@@ -63,12 +61,15 @@ def tile_list_meltab_maglog_kernel(
         table = keep.tile([P, T], I32, name="table", align_bytes=64)
         nc.sync.dma_start(table[:], tab_words[0].rearrange("p t b -> p (t b)").bitcast(I32))
 
-        nc.vector.memset(table_scales[:].bitcast(I32)[0:96, :], 0)
-        nc.gpsimd.memset(weight_scales[:].bitcast(I32)[0:96], 0)
-        first_planes = keep.tile([P, PASSES, FIRST_W], U8, name="first_planes", align_bytes=64)
+        for dead in (slice(32, 64), slice(64, P)):
+            nc.vector.memset(table_scales[:].bitcast(I32)[dead], 0)
+            nc.gpsimd.memset(weight_scales[:].bitcast(I32)[dead], 0)
+        first_planes = [
+            keep.tile([P, FIRST_W], U8, name="first_plane%d" % a, align_bytes=64) for a in range(PASSES)
+        ]
         middle_planes = keep.tile([P, PASSES, 2 * JT], U8, name="middle_planes", align_bytes=64)
         last_planes = keep.tile([P, PASSES, JT], U8, name="last_planes", align_bytes=64)
-        nc.gpsimd.memset(first_planes[:].bitcast(I32), 0)
+        nc.gpsimd.memset(first_planes[1][:].bitcast(I32), 0)
         nc.gpsimd.memset(middle_planes[:].bitcast(I32), 0)
         nc.gpsimd.memset(last_planes[:].bitcast(I32), 0)
 
@@ -83,26 +84,27 @@ def tile_list_meltab_maglog_kernel(
         def gather_scales(dst, c):
             nc.vector.tensor_copy(dst, table_scales[:].indirect(list_slice(c)))
 
-        def place_rows(queue, planes, source, widths):
+        def place_rows(queue, plane, source, a, q):
+            row = 16 * a + 4 * q
+            queue.dma_start(plane.bitcast(I32)[32 * q : 32 * q + 4, :], source[:].bitcast(I32)[row : row + 4, :])
+
+        def place_all(planes, source):
             for a in range(PASSES):
                 for q in range(4):
-                    row = 96 + 16 * a + 4 * q
-                    queue.dma_start(
-                        planes[:, a, : widths[a]].bitcast(I32)[32 * q : 32 * q + 4, :],
-                        source[:, : widths[a]].bitcast(I32)[row : row + 4, :],
-                    )
+                    place_rows(nc.sync, planes[:, a, :], source, a, q)
 
-        def permute_words(name, raw_words):
-            codes = keep.tile([P, PASSES, PACK, P], I32, name=name, align_bytes=64)
+        def permute_words(codes, raw_words):
             for a in range(PASSES):
                 nc.vector.tensor_copy(
                     codes[:, a].rearrange("p t (u i) -> p u t i", i=4),
                     raw_words[:, a].rearrange("p (u i t) -> p u t i", i=4, t=PACK),
                 )
-            return codes
 
         def gather_frames(c):
-            picked = ring.tile([P, JT], U32, name="picked", align_bytes=64, bufs=1)
+            if c == 0:
+                picked = handed.tile([P, JT], U32, name="first_picked", align_bytes=64, offset=1024)
+            else:
+                picked = handed.tile([P, JT], U32, name="picked", align_bytes=64, offset=0)
             nc.vector.tensor_copy(picked[:], table[:].bitcast(U32).indirect(list_slice(c)))
             frames = ring.tile([P, PASSES, 2 * JT], U8, name="frames", align_bytes=64)
             nc.vector.tensor_copy(
@@ -113,30 +115,38 @@ def tile_list_meltab_maglog_kernel(
         first_scales = keep.tile([P, JT], U8, name="first_scales", align_bytes=64)
         gather_scales(first_scales[:], 0)
         nc.vector.tensor_copy(
-            first_rows[:, : 2 * F].rearrange("p (w t m) -> p w t m", w=2, t=PACK),
+            first_planes[0][:, : 2 * F].rearrange("p (w t m) -> p w t m", w=2, t=PACK),
             weight_scales[:].rearrange("p w (m t) -> p w t m", t=PACK),
         )
-        nc.vector.tensor_copy(
-            first_rows[:, FRAMES_AT:FB_AT].bitcast(I32)[rows, :], first_scales[:].bitcast(I32)[rows, :]
-        )
-        place_rows(nc.scalar, first_planes, first_rows, (FIRST_W, FB_AT))
-        co_codes = permute_words("co_codes", co_raw)
+        nc.vector.tensor_copy(first_planes[0][:, FRAMES_AT:].bitcast(I32), first_scales[:].bitcast(I32))
+        for a in range(PASSES):
+            for q in range(4):
+                if (a, q) != (0, 0):
+                    place_rows(nc.scalar, first_planes[a][:], first_planes[0], a, q)
+        co_codes = keep.tile([P, PASSES, PACK, P], I32, name="co_codes", align_bytes=64)
+        permute_words(co_codes, co_raw)
         si_raw = keep.tile([P, PASSES, F], I32, name="si_raw", tag="staging", align_bytes=64)
-        nc.sync.dma_start(si_raw[:], words_view(si_words))
+        nc.scalar.dma_start(si_raw[:], words_view(si_words))
         frames_next = gather_frames(0)
-        si_codes = permute_words("si_codes", si_raw)
+        si_codes = handed.tile([P, PASSES, PACK, P], I32, name="si_codes", align_bytes=64, offset=2048)
+        permute_words(si_codes, si_raw)
         middle_scales = keep.tile([P, 2 * JT], U8, name="middle_scales", align_bytes=64)
         for c in (1, 2):
             gather_scales(middle_scales[:, (c - 1) * JT : c * JT], c)
-        place_rows(nc.sync, middle_planes, middle_scales, (2 * JT, 2 * JT))
+        place_all(middle_planes, middle_scales)
         last_scales = keep.tile([P, JT], U8, name="last_scales", tag="staging", align_bytes=64)
         gather_scales(last_scales[:], 3)
-        place_rows(nc.sync, last_planes, last_scales, (JT, JT))
+        place_all(last_planes, last_scales)
         co = (co_codes, 0)
         si = (si_codes, F)
 
-        fb_codes = keep.tile([P, N], I32, name="fb_codes", tag="staging", align_bytes=64)
-        nc.sync.dma_start(fb_codes[:], fb_words[0].rearrange("p n b -> p (n b)").bitcast(I32))
+        fb_bytes = keep.tile([P, N * (PACK + 1)], U8, name="fb_bytes", tag="staging", align_bytes=64)
+        fb_codes = fb_bytes[:, : N * PACK].bitcast(I32)
+        fb_plane = fb_bytes[:, N * PACK :]
+        nc.vector.memset(fb_plane.bitcast(I32), 0)
+        nc.sync.dma_start(fb_codes, fb_words[0].rearrange("p n b -> p (n b)").bitcast(I32))
+        for q in range(4):
+            nc.sync.dma_start(fb_plane.bitcast(I32)[32 * q : 32 * q + 4, :], rows_view(fb_scales)[4 * q : 4 * q + 4, :])
 
         sign_col = keep.tile([P, PACK], F32, name="sign_col")
         nc.vector.tensor_scalar(sign_col[:], gain[:], 0.0, 2.0, ALU.is_ge, ALU.mult)
@@ -144,14 +154,13 @@ def tile_list_meltab_maglog_kernel(
         nc.vector.tensor_scalar(
             signs[:], sign_col[:].unsqueeze(1).to_broadcast([P, SIGN_COLS, PACK]), -1.0, None, ALU.add
         )
-        sign_rows = signs[:].rearrange("p j t -> p (j t)").unsqueeze(1)
-        sign_rows = sign_rows.to_broadcast([P, JT // SIGN_COLS, SIGN_COLS * PACK])
+        sign_row = signs[:].rearrange("p j t -> p (j t)").unsqueeze(1)
 
         def transform(acc, weight, frames, c, t):
             codes, at = weight
             for a in range(PASSES):
                 if c == 0:
-                    frame_plane = first_planes[:, a, FRAMES_AT:FB_AT]
+                    frame_plane = first_planes[a][:, FRAMES_AT:]
                 elif c < 3:
                     frame_plane = middle_planes[:, a, (c - 1) * JT : c * JT]
                 else:
@@ -159,7 +168,7 @@ def tile_list_meltab_maglog_kernel(
                 nc.tensor.matmul_mx(
                     out=acc,
                     lhsT=codes[:, a, t, :].bitcast(FP8X4),
-                    lhsT_scale=first_planes[:, a, at + t * P : at + (t + 1) * P],
+                    lhsT_scale=first_planes[a][:, at + t * P : at + (t + 1) * P],
                     rhs=frames[:, a, :].bitcast(FP4X4),
                     rhs_scale=frame_plane,
                     start=(a == 0),
@@ -202,14 +211,14 @@ def tile_list_meltab_maglog_kernel(
                     if c > 0:
                         transform(re[t], co, frames, c, t)
                     transform(im[t], si, frames, c, t)
-                on_vector = (c, u) in VECTOR_PAIRS
+                on_vector = [t for t in pair if (c, t) in VECTOR_SQUARES]
                 if on_vector:
-                    im_g = ring.tile([P, 2, JT], F32, name="im_g")
-                    for t in pair:
-                        nc.vector.tensor_scalar(im_g[:, t % 2, :], im[t], gain[:, t : t + 1], None, ALU.mult)
-                    nc.vector.tensor_tensor(sq[:, both, 1, :], im_g[:], im_g[:], ALU.mult)
+                    im_g = ring.tile([P, len(on_vector), JT], F32, name="im_g")
+                    for k, t in enumerate(on_vector):
+                        nc.vector.tensor_scalar(im_g[:, k, :], im[t], gain[:, t : t + 1], None, ALU.mult)
+                    nc.vector.tensor_tensor(sq[:, on_vector[0] : on_vector[-1] + 1, 1, :], im_g[:], im_g[:], ALU.mult)
                 for t in (pair if c == 0 else reversed(pair)):
-                    if not on_vector:
+                    if t not in on_vector:
                         square(sq[:, t, 1, :], im[t], t)
                     if c > 0:
                         square(sq[:, t, 0, :], re[t], t)
@@ -226,29 +235,36 @@ def tile_list_meltab_maglog_kernel(
             root(c, 1)
 
         result = keep.tile([P, N // P, J], F32, name="result", tag="power%d" % (TILES - 1))
-        for c in range(TILES):
-            h = ring.tile([P, JT * PACK], BF16, name="h", align_bytes=64)
+        pieces = [(c * JT, JT) for c in range(TILES - 1)] + [(J - JT, JT // 2), (J - JT // 2, JT // 2)]
+        bank = 0
+        for j0, width in pieces:
+            c, at = divmod(j0, JT)
+            h = ring.tile([P, width * PACK], BF16, name="h", align_bytes=64)
             nc.vector.tensor_tensor(
                 h[:].rearrange("p (u x) -> p u x", x=SIGN_COLS * PACK),
-                magnitude[c][:].rearrange("p (u j) t -> p u (j t)", j=SIGN_COLS),
-                sign_rows,
+                magnitude[c][:, at : at + width, :].rearrange("p (u j) t -> p u (j t)", j=SIGN_COLS),
+                sign_row.to_broadcast([P, width // SIGN_COLS, SIGN_COLS * PACK]),
                 ALU.mult,
             )
-            h_codes = ring.tile([P, JT], U32, name="h_codes", align_bytes=64, bufs=4)
-            h_plane = ring.tile([P, JT], U8, name="h_plane", align_bytes=64, bufs=4)
+            h_codes = ring.tile([P, width], U32, name="h_codes", align_bytes=64, bufs=4)
+            h_plane = ring.tile([P, width], U8, name="h_plane", align_bytes=64, bufs=4)
             nc.vector.quantize_mx(out=h_codes[:].bitcast(FP8X4), scales=h_plane[:], in_=h[:])
-            ys = [psum.tile([P, JT], F32, name="y", tag="bank%d" % (2 * c + n))[:] for n in range(N // P)]
-            for n in range(N // P):
-                nc.tensor.matmul_mx(
-                    out=ys[n],
-                    lhsT=fb_codes[:, n * P : (n + 1) * P].bitcast(FP8X4),
-                    lhsT_scale=first_planes[:, 0, FB_AT + n * P : FB_AT + (n + 1) * P],
-                    rhs=h_codes[:].bitcast(FP8X4),
-                    rhs_scale=h_plane[:],
-                    start=True,
-                    stop=True,
-                )
-            cols = slice(c * JT, (c + 1) * JT)
-            for n in reversed(range(N // P)):
-                nc.scalar.activation(result[:, n, cols], ys[n], ACT.Ln, bias=1.0)
-                nc.sync.dma_start(out[n * P : (n + 1) * P, cols], result[:, n, cols])
+            per_bank = JT // width
+            cols = slice(j0, j0 + width)
+            for n0 in range(0, N // P, per_bank):
+                y = psum.tile([P, per_bank, width], F32, name="y", tag="bank%d" % bank)
+                bank += 1
+                for k in range(per_bank):
+                    n = n0 + k
+                    nc.tensor.matmul_mx(
+                        out=y[:, k, :],
+                        lhsT=fb_codes[:, n * P : (n + 1) * P].bitcast(FP8X4),
+                        lhsT_scale=fb_plane[:, n * P : (n + 1) * P],
+                        rhs=h_codes[:].bitcast(FP8X4),
+                        rhs_scale=h_plane[:],
+                        start=True,
+                        stop=True,
+                    )
+                blocks = slice(n0, n0 + per_bank)
+                nc.scalar.activation(result[:, blocks, cols], y[:], ACT.Ln, bias=1.0)
+                nc.sync.dma_start(out.rearrange("(n p) j -> p n j", p=P)[:, blocks, cols], result[:, blocks, cols])

from contextlib import ExitStack

import concourse.mybir as mybir

K, F, N, T, J = 1024, 512, 256, 4096, 2048
FLOPS = 2 * 2 * K * F * J + 2 * F * N * J

F32 = mybir.dt.float32
BF16 = mybir.dt.bfloat16
I32 = mybir.dt.int32
U32 = mybir.dt.uint32
U16 = mybir.dt.uint16
U8 = mybir.dt.uint8
FP8X4 = mybir.dt.float8_e4m3fn_x4
FP4X4 = mybir.dt.float4_e2m1fn_x4
ALU = mybir.AluOpType
ACT = mybir.ActivationFunctionType

P = 128
PACK = 4
PASSES = K // (P * PACK)
JT = 512
TILES = J // JT
RUN = 2
SIGN_COLS = 32
FRAMES_AT = 2 * F
FIRST_W = FRAMES_AT + JT
VECTOR_SQUARES = ((1, 3), (2, 2), (2, 3), (3, 0), (3, 1))


def tile_list_meltab_maglog_kernel(
    tc, tab_words, tab_scales, co_words, co_scales, si_words, si_scales, gn, fb_words, fb_scales, offs, out
):
    nc = tc.nc
    with ExitStack() as ctx:
        keep = ctx.enter_context(tc.tile_pool(name="keep", bufs=1))
        handed = ctx.enter_context(tc.tile_pool(name="handed", bufs=1))
        ring = ctx.enter_context(tc.tile_pool(name="ring", bufs=2))
        psum = ctx.enter_context(tc.psum_pool(name="psum", bufs=1))

        offsets = keep.tile([P, J // 16], U16, name="offsets")
        nc.sync.dma_start(offsets[:], offs)

        rows = slice(0, 32)

        def words_view(words):
            return words.rearrange("a p f b -> p a (f b)").bitcast(I32)

        def rows_view(scales):
            return scales.rearrange("a q c -> (a q) c").bitcast(I32)

        table_scales = keep.tile([P, T], U8, name="table_scales", align_bytes=64)
        nc.sync.dma_start(table_scales[:].bitcast(I32)[rows, :], rows_view(tab_scales))
        weight_scales = keep.tile([P, 2, F], U8, name="weight_scales", align_bytes=64)
        nc.sync.dma_start(weight_scales[:, 0, :].bitcast(I32)[rows, :], rows_view(co_scales))
        nc.sync.dma_start(weight_scales[:, 1, :].bitcast(I32)[rows, :], rows_view(si_scales))
        gain = keep.tile([P, PACK], F32, name="gain")
        nc.sync.dma_start(gain[:], gn.rearrange("(p t) -> p t", t=PACK))
        co_raw = keep.tile([P, PASSES, F], I32, name="co_raw", tag="staging", align_bytes=64)
        nc.sync.dma_start(co_raw[:], words_view(co_words))
        table = keep.tile([P, T], I32, name="table", align_bytes=64)
        nc.sync.dma_start(table[:], tab_words[0].rearrange("p t b -> p (t b)").bitcast(I32))

        for dead in (slice(32, 64), slice(64, P)):
            nc.vector.memset(table_scales[:].bitcast(I32)[dead], 0)
            nc.gpsimd.memset(weight_scales[:].bitcast(I32)[dead], 0)
        first_planes = [
            keep.tile([P, FIRST_W], U8, name="first_plane%d" % a, align_bytes=64) for a in range(PASSES)
        ]
        middle_planes = keep.tile([P, PASSES, 2 * JT], U8, name="middle_planes", align_bytes=64)
        last_planes = keep.tile([P, PASSES, JT], U8, name="last_planes", align_bytes=64)
        nc.gpsimd.memset(first_planes[1][:].bitcast(I32), 0)
        nc.gpsimd.memset(middle_planes[:].bitcast(I32), 0)
        nc.gpsimd.memset(last_planes[:].bitcast(I32), 0)

        zero_in = keep.tile([P, 1], F32, name="zero_in")
        zero = keep.tile([P, 1], F32, name="zero")
        nc.vector.memset(zero_in[:], 0.0)
        nc.scalar.activation(zero[:], zero_in[:], ACT.Sqrt)

        def list_slice(c):
            return offsets[:, c * (JT // 16) : (c + 1) * (JT // 16)]

        def gather_scales(dst, c):
            nc.vector.tensor_copy(dst, table_scales[:].indirect(list_slice(c)))

        def place_rows(queue, plane, source, a, q):
            row = 16 * a + 4 * q
            queue.dma_start(plane.bitcast(I32)[32 * q : 32 * q + 4, :], source[:].bitcast(I32)[row : row + 4, :])

        def place_all(planes, source):
            for a in range(PASSES):
                for q in range(4):
                    place_rows(nc.sync, planes[:, a, :], source, a, q)

        def permute_words(codes, raw_words):
            for a in range(PASSES):
                nc.vector.tensor_copy(
                    codes[:, a].rearrange("p t (u i) -> p u t i", i=4),
                    raw_words[:, a].rearrange("p (u i t) -> p u t i", i=4, t=PACK),
                )

        def gather_frames(c):
            if c == 0:
                picked = handed.tile([P, JT], U32, name="first_picked", align_bytes=64, offset=1024)
            else:
                picked = handed.tile([P, JT], U32, name="picked", align_bytes=64, offset=0)
            nc.vector.tensor_copy(picked[:], table[:].bitcast(U32).indirect(list_slice(c)))
            frames = ring.tile([P, PASSES, 2 * JT], U8, name="frames", align_bytes=64)
            nc.vector.tensor_copy(
                frames[:].bitcast(U16), picked[:].bitcast(U16).rearrange("p (j d) -> p d j", d=PASSES)
            )
            return frames

        first_scales = keep.tile([P, JT], U8, name="first_scales", align_bytes=64)
        gather_scales(first_scales[:], 0)
        nc.vector.tensor_copy(
            first_planes[0][:, : 2 * F].rearrange("p (w t m) -> p w t m", w=2, t=PACK),
            weight_scales[:].rearrange("p w (m t) -> p w t m", t=PACK),
        )
        nc.vector.tensor_copy(first_planes[0][:, FRAMES_AT:].bitcast(I32), first_scales[:].bitcast(I32))
        for a in range(PASSES):
            for q in range(4):
                if (a, q) != (0, 0):
                    place_rows(nc.scalar, first_planes[a][:], first_planes[0], a, q)
        co_codes = keep.tile([P, PASSES, PACK, P], I32, name="co_codes", align_bytes=64)
        permute_words(co_codes, co_raw)
        si_raw = keep.tile([P, PASSES, F], I32, name="si_raw", tag="staging", align_bytes=64)
        nc.scalar.dma_start(si_raw[:], words_view(si_words))
        frames_next = gather_frames(0)
        si_codes = handed.tile([P, PASSES, PACK, P], I32, name="si_codes", align_bytes=64, offset=2048)
        permute_words(si_codes, si_raw)
        middle_scales = keep.tile([P, 2 * JT], U8, name="middle_scales", align_bytes=64)
        for c in (1, 2):
            gather_scales(middle_scales[:, (c - 1) * JT : c * JT], c)
        place_all(middle_planes, middle_scales)
        last_scales = keep.tile([P, JT], U8, name="last_scales", tag="staging", align_bytes=64)
        gather_scales(last_scales[:], 3)
        place_all(last_planes, last_scales)
        co = (co_codes, 0)
        si = (si_codes, F)

        fb_bytes = keep.tile([P, N * (PACK + 1)], U8, name="fb_bytes", tag="staging", align_bytes=64)
        fb_codes = fb_bytes[:, : N * PACK].bitcast(I32)
        fb_plane = fb_bytes[:, N * PACK :]
        nc.vector.memset(fb_plane.bitcast(I32), 0)
        nc.sync.dma_start(fb_codes, fb_words[0].rearrange("p n b -> p (n b)").bitcast(I32))
        for q in range(4):
            nc.sync.dma_start(fb_plane.bitcast(I32)[32 * q : 32 * q + 4, :], rows_view(fb_scales)[4 * q : 4 * q + 4, :])

        sign_col = keep.tile([P, PACK], F32, name="sign_col")
        nc.vector.tensor_scalar(sign_col[:], gain[:], 0.0, 2.0, ALU.is_ge, ALU.mult)
        signs = keep.tile([P, SIGN_COLS, PACK], BF16, name="signs", align_bytes=64)
        nc.vector.tensor_scalar(
            signs[:], sign_col[:].unsqueeze(1).to_broadcast([P, SIGN_COLS, PACK]), -1.0, None, ALU.add
        )
        sign_row = signs[:].rearrange("p j t -> p (j t)").unsqueeze(1)

        def transform(acc, weight, frames, c, t):
            codes, at = weight
            for a in range(PASSES):
                if c == 0:
                    frame_plane = first_planes[a][:, FRAMES_AT:]
                elif c < 3:
                    frame_plane = middle_planes[:, a, (c - 1) * JT : c * JT]
                else:
                    frame_plane = last_planes[:, a, :]
                nc.tensor.matmul_mx(
                    out=acc,
                    lhsT=codes[:, a, t, :].bitcast(FP8X4),
                    lhsT_scale=first_planes[a][:, at + t * P : at + (t + 1) * P],
                    rhs=frames[:, a, :].bitcast(FP4X4),
                    rhs_scale=frame_plane,
                    start=(a == 0),
                    stop=(a == PASSES - 1),
                )

        squares = []
        power = []
        magnitude = []

        def root(c, half):
            cols = slice(half * (JT // 2), (half + 1) * (JT // 2))
            nc.scalar.activation(
                magnitude[c][:, cols, :].rearrange("p j (u e) -> p j u e", e=2),
                power[c][:, :, cols, :].rearrange("p u j e -> p j u e"),
                ACT.Sqrt,
                bias=zero[:],
            )

        def square(dst, src, t):
            nc.scalar.activation(dst, src, ACT.Square, scale=gain[:, t : t + 1])

        for c in range(TILES):
            frames = frames_next
            if c + 1 < TILES:
                frames_next = gather_frames(c + 1)
            sq = keep.tile([P, PACK, 2, JT], F32, name="sq", tag="squares%d" % (c % 2))
            power.append(keep.tile([P, PACK // 2, JT, 2], F32, name="power", tag="power%d" % c))
            magnitude.append(keep.tile([P, JT, PACK], BF16, name="magnitude", tag="magnitude%d" % c, align_bytes=64))
            re = [psum.tile([P, JT], F32, name="re", tag="bank%d" % (2 * t))[:] for t in range(PACK)]
            im = [psum.tile([P, JT], F32, name="im", tag="bank%d" % (2 * t + 1))[:] for t in range(PACK)]
            if c == 0:
                for t in range(PACK):
                    transform(re[t], co, frames, c, t)
                    square(sq[:, t, 0, :], re[t], t)
            for u in range(PACK // 2):
                pair = (2 * u, 2 * u + 1)
                both = slice(2 * u, 2 * u + 2)
                for t in pair:
                    if c > 0:
                        transform(re[t], co, frames, c, t)
                    transform(im[t], si, frames, c, t)
                on_vector = [t for t in pair if (c, t) in VECTOR_SQUARES]
                if on_vector:
                    im_g = ring.tile([P, len(on_vector), JT], F32, name="im_g")
                    for k, t in enumerate(on_vector):
                        nc.vector.tensor_scalar(im_g[:, k, :], im[t], gain[:, t : t + 1], None, ALU.mult)
                    nc.vector.tensor_tensor(sq[:, on_vector[0] : on_vector[-1] + 1, 1, :], im_g[:], im_g[:], ALU.mult)
                for t in (pair if c == 0 else reversed(pair)):
                    if t not in on_vector:
                        square(sq[:, t, 1, :], im[t], t)
                    if c > 0:
                        square(sq[:, t, 0, :], re[t], t)
                nc.vector.tensor_tensor(
                    power[c][:, u].rearrange("p (v i) e -> p v e i", i=RUN),
                    sq[:, both, 0, :].rearrange("p e (v i) -> p v e i", i=RUN),
                    sq[:, both, 1, :].rearrange("p e (v i) -> p v e i", i=RUN),
                    ALU.add,
                )
                if 0 < c < TILES - 1:
                    root(c - 1, u)
        for c in (TILES - 2, TILES - 1):
            root(c, 0)
            root(c, 1)

        result = keep.tile([P, N // P, J], F32, name="result", tag="power%d" % (TILES - 1))
        pieces = [(c * JT, JT) for c in range(TILES - 1)] + [(J - JT, JT // 2), (J - JT // 2, JT // 2)]
        bank = 0
        for j0, width in pieces:
            c, at = divmod(j0, JT)
            h = ring.tile([P, width * PACK], BF16, name="h", align_bytes=64)
            nc.vector.tensor_tensor(
                h[:].rearrange("p (u x) -> p u x", x=SIGN_COLS * PACK),
                magnitude[c][:, at : at + width, :].rearrange("p (u j) t -> p u (j t)", j=SIGN_COLS),
                sign_row.to_broadcast([P, width // SIGN_COLS, SIGN_COLS * PACK]),
                ALU.mult,
            )
            h_codes = ring.tile([P, width], U32, name="h_codes", align_bytes=64, bufs=4)
            h_plane = ring.tile([P, width], U8, name="h_plane", align_bytes=64, bufs=4)
            nc.vector.quantize_mx(out=h_codes[:].bitcast(FP8X4), scales=h_plane[:], in_=h[:])
            per_bank = JT // width
            cols = slice(j0, j0 + width)
            for n0 in range(0, N // P, per_bank):
                y = psum.tile([P, per_bank, width], F32, name="y", tag="bank%d" % bank)
                bank += 1
                for k in range(per_bank):
                    n = n0 + k
                    nc.tensor.matmul_mx(
                        out=y[:, k, :],
                        lhsT=fb_codes[:, n * P : (n + 1) * P].bitcast(FP8X4),
                        lhsT_scale=fb_plane[:, n * P : (n + 1) * P],
                        rhs=h_codes[:].bitcast(FP8X4),
                        rhs_scale=h_plane[:],
                        start=True,
                        stop=True,
                    )
                blocks = slice(n0, n0 + per_bank)
                nc.scalar.activation(result[:, blocks, cols], y[:], ACT.Ln, bias=1.0)
                nc.sync.dma_start(out.rearrange("(n p) j -> p n j", p=P)[:, blocks, cols], result[:, blocks, cols])
